import numpy as np, ml_dtypes
CORES = [49,52,55,57,60,63,65,68,71,73,76,79]
N = 12
NH, QP = 2, 128
def setup_inputs(rng):
    q = rng.standard_normal((N, 128, NH * QP), dtype=np.float32) / 4; k = rng.standard_normal((N, 128, NH * 128), dtype=np.float32)
    a = 2 * np.pi * rng.random((N, NH * QP)); s = 400 * rng.random((N, NH * QP)) ** 1.5; q[:, 0, :] = s * np.cos(a); q[:, 1, :] = s * np.sin(a); q[:, 2, :] = 150 * rng.standard_normal((N, NH * QP)); k[:, 2, :] = 1 + k[:, 2, :] / 50
    a = (2 * np.pi * rng.random((1, NH, 1)) + np.pi / 2 * (rng.permuted(np.tile(np.arange(N), (NH, 1)), axis=1).T.reshape(N, NH, 1) + 0.5) / N - 0.5 + rng.random((N, NH, 128))).reshape(N, NH * 128); k[:, 0, :] = np.cos(a); k[:, 1, :] = np.sin(a)
    return {"q": q.astype(ml_dtypes.bfloat16), "k": k.astype(ml_dtypes.bfloat16), "v": rng.standard_normal((N, 128, NH * 128), dtype=np.float32).astype(ml_dtypes.bfloat16)}
def setup_inputs_big(rng):
    d = setup_inputs(rng)
    for k in ("v",): d[k] = (d[k].astype(np.float32) * 1048576.0).astype(d[k].dtype)
    return d
def setup_inputs_small(rng):
    d = setup_inputs(rng)
    for k in ("v",): d[k] = (d[k].astype(np.float32) * (1 / 1048576.0)).astype(d[k].dtype)
    return d
def reference(q, k, v):
    Q, K, V = q.astype(np.float64), k.astype(np.float64), v.astype(np.float64)
    y = np.zeros((N, QP, NH * 128))
    for r in range(N):
        for h in range(NH):
            S = np.concatenate([K[j][:, 128 * h:128 * h + 128].T @ Q[r][:, QP * h:QP * h + QP] for j in range(N)], axis=0)
            P = np.exp(S - S.max(axis=0)); P = P / P.sum(axis=0)
            y[r][:, 128 * h:128 * h + 128] = P.T @ np.concatenate([V[j][:, 128 * h:128 * h + 128] for j in range(N)], axis=0)
    return {"y": y.astype(ml_dtypes.bfloat16)}

@@ -1,0 +1,365 @@
+from concourse.bass import DstId, RemoteDMATransfer
+from concourse.mybir import AluOpType, AxisListType, ActivationFunctionType
+
+BF, F32 = "bfloat16", "float32"
+SCRATCH = {
+    "kvown": ("sbuf", [128, 512], BF),
+    "qs": ("sbuf", [128, 256], BF),
+    "kv": ("sbuf", [128, 6 * 256], BF),
+    "qin": ("sbuf", [128, 512], BF),
+    "qrel": ("sbuf", [128, 256], BF),
+    "ones": ("sbuf", [128, 128], BF),
+    "ident": ("sbuf", [128, 128], BF),
+    "sb": ("sbuf", [128, 16], BF),
+    "sf": ("sbuf", [128, 32], F32),
+    "ysb": ("sbuf", [128, 256], BF),
+}
+for _q in range(2):
+    SCRATCH["os%d" % _q] = ("sbuf", [128, 136], BF)
+    SCRATCH["oin%d" % _q] = ("sbuf", [128, 272], BF)
+    SCRATCH["ol%d" % _q] = ("sbuf", [128, 128], F32)
+    SCRATCH["ta%d" % _q] = ("sbuf", [128, 128], F32)
+    SCRATCH["tb%d" % _q] = ("sbuf", [128, 128], F32)
+    SCRATCH["PT%d" % _q] = ("psum", [128, 1024], BF)
+    SCRATCH["O%d" % _q] = ("psum", [128, 512], F32)
+    for _g in range(2):
+        SCRATCH["p%d%d" % (_q, _g)] = ("sbuf", [128, 512], BF)
+        SCRATCH["pt%d%d" % (_q, _g)] = ("sbuf", [128, 512], BF)
+        SCRATCH["S%d%d" % (_q, _g)] = ("psum", [128, 512], F32)
+
+SEMAPHORES = ["ld_kv", "ld_q", "kl", "kd", "kf", "qa0", "qa1", "qr", "oa0", "oa1", "snd", "st", "on", "id", "c0", "c1"]
+for _q in range(2):
+    SEMAPHORES += ["%s%d" % (s, _q) for s in ("sN", "sA", "sL", "sF")]
+    for _g in range(2):
+        SEMAPHORES += ["%s%d%d" % (s, _q, _g) for s in ("sS", "sM", "sE", "sT", "sC", "sO")]
+
+
+def _bits(m):
+    return [e for e in range(m.bit_length()) if (m >> e) & 1]
+
+
+def _plan(T, topo):
+    cores = list(T.cores)
+    chips = sorted(set(topo.chip(c) for c in cores))
+    P = {}
+    for X in chips:
+        ranks = [c for c in cores if topo.chip(c) == X]
+        mate = [Y for Y in chips if topo.mates(X, Y)][0]
+        plane = [Y for Y in chips if topo.same_plane(X, Y)][0]
+        probe = [c for c in cores if topo.chip(c) == mate][0]
+        owners = [c for c in range(topo.CHIPS * topo.CORES_PER_CHIP) if topo.chip(c) == X and topo.may_write(c, probe)]
+        NP = [r for r in ranks if r not in owners]
+        PR = [r for r in ranks if r in owners][0]
+        W = []
+        for h in range(2):
+            od = [c for c in owners if topo.die(c) == topo.die(NP[h])]
+            B = PR if PR in od else od[-1]
+            A = [c for c in od if c != B][0]
+            W.append([NP[h], A, B])
+        P[X] = dict(ranks=ranks, mate=mate, plane=plane, NP=NP, PR=PR, W=W)
+    return P
+
+
+def _role(c, P, topo):
+    X = topo.chip(c)
+    if X not in P:
+        return None
+    for h in range(2):
+        for i, w in enumerate(P[X]["W"][h]):
+            if w == c:
+                return (h, i)
+    return None
+
+
+def _blocks(c, P, topo):
+    me = P[topo.chip(c)]
+    M = P[me["mate"]]
+    h, i = _role(c, P, topo)
+    if i == 0:
+        return [(me["NP"][1 - h], "own"), (me["NP"][h], "own")]
+    if i == 1:
+        return [(M["PR"], "mate"), (M["NP"][h], "mate")]
+    return [(me["PR"], "own"), (M["NP"][1 - h], "mate")]
+
+
+def _sends(c, P, topo):
+    me = P[topo.chip(c)]
+    M, PL = P[me["mate"]], P[me["plane"]]
+    h, i = _role(c, P, topo)
+    lo = _bits(topo.mask(c, M["ranks"][0]))
+    on = _bits(topo.mask(c, [w for w in me["W"][0] + me["W"][1] if w != c][0]))
+    hi = [e for e in on if e not in lo]
+    hl, hh_ = len(lo) // 2, len(hi) // 2
+    calls = {}
+    if c in me["ranks"]:
+        r = me["ranks"].index(c)
+        calls["kvx"] = [dict(src=("kvown", k * 256, k * 256 + 256),
+                             dsts=[(PL["W"][k][r], "kv", (3 + r) * 256, (4 + r) * 256)],
+                             sem="kd", eng=lo[k * hl:(k + 1) * hl]) for k in range(2)]
+        if c != me["PR"]:
+            calls["q"] = [dict(src=("qs", 0, 256), dsts=[(me["W"][h][1], "qrel", 0, 256)], sem="qr", eng=hi[:hh_]),
+                          dict(src=("qs", 0, 256), dsts=[(me["W"][1 - h][0], "qin", 0, 256)], sem="qa0", eng=hi[hh_:])]
+        else:
+            t = []
+            for k in range(2):
+                t.append(dict(src=("qs", k * 128, k * 128 + 128), dsts=[(M["W"][k][1], "qin", k * 128, k * 128 + 128)],
+                              sem="qa0", eng=lo[k * hl:(k + 1) * hl]))
+                if me["W"][k][2] != c:
+                    t.append(dict(src=("qs", k * 128, k * 128 + 128),
+                                  dsts=[(me["W"][k][2], "qin", k * 128, k * 128 + 128)], sem="qa0", eng=hi))
+            calls["q"] = t
+        t = []
+        for k in range(2):
+            d = [w for w in me["W"][k] if w != c]
+            t.append(dict(src=("kvown", k * 256, k * 256 + 256), dsts=[(w, "kv", r * 256, (r + 1) * 256) for w in d],
+                          sem="kl", eng=hi if len(d) == 3 else lo))
+        calls["kvl"] = t
+    if i == 1:
+        calls["qrel"] = [dict(src=("qrel", k * 128, k * 128 + 128),
+                              dsts=[(M["W"][k][1] if k == h else M["W"][k][2], "qin", 256 + k * 128, 384 + k * 128)],
+                              sem="qa1", eng=lo[k * hl:(k + 1) * hl]) for k in range(2)]
+    others = [w for w in me["W"][h] if w != c]
+    calls["fwd"] = [dict(src=("kv", (3 + i) * 256, (4 + i) * 256), dsts=[(others[k], "kv", (3 + i) * 256, (4 + i) * 256)],
+                         sem="kf", eng=(lo, hi)[k]) for k in range(2)]
+    for b, (owner, kind) in enumerate(_blocks(c, P, topo)):
+        if owner != c:
+            off = 0 if kind == "own" else 136
+            calls["o%d" % b] = [dict(src=("os%d" % b, 0, 130), dsts=[(owner, "oin%d" % h, off, off + 130)],
+                                     sem="oa%d" % h, eng=(lo + hi) if topo.chip(owner) == topo.chip(c) else lo)]
+    return calls
+
+
+def rank_program(g, core, T, topo):
+    P = _plan(T, topo)
+    role = _role(core, P, topo)
+    if role is None:
+        return
+    h, i = role
+    me = P[topo.chip(core)]
+    isrank = core in me["ranks"]
+    blocks = _blocks(core, P, topo)
+    calls = _sends(core, P, topo)
+    pe, dv, ac, sy = g.tensor, g.vector, g.scalar, g.sync
+    Exp, Copy, X = ActivationFunctionType.Exp, ActivationFunctionType.Copy, AxisListType.X
+    A = AluOpType
+
+    tot = {}
+    for Y in P:
+        for k in range(2):
+            for w in P[Y]["W"][k]:
+                if w == core:
+                    continue
+                for trs in _sends(w, P, topo).values():
+                    for t in trs:
+                        for d in t["dsts"]:
+                            if d[0] == core:
+                                tot[t["sem"]] = tot.get(t["sem"], 0) + len(t["eng"])
+
+    def S(n):
+        return T.sem[n]
+
+    def inc(ins, n, k=1):
+        ins.then_inc(S(n), k)
+        tot[n] = tot.get(n, 0) + k
+
+    def need(q, *names):
+        for n in names:
+            if tot.get(n, 0) > 0:
+                q.wait_ge(S(n), tot[n])
+
+    def emit(name):
+        trs = []
+        for t in calls[name]:
+            b, c0, c1 = t["src"]
+            ids, dsts = [], []
+            for (dc, db, d0, d1) in t["dsts"]:
+                rid, pid, _se = topo.addr(dc)
+                ids.append(DstId(rid=rid, pnc=pid))
+                dsts.append(T[db][:, d0:d1])
+            trs.append(RemoteDMATransfer(dst_ids=ids, dma_engine_mask=sum(1 << e for e in t["eng"]), remote_sem=S(t["sem"]),
+                                         srcs=[T[b][:, c0:c1]], dsts=dsts, alu_op=0))
+            tot["snd"] = tot.get("snd", 0) + len(t["eng"])
+        g.remote_dma_fused(trs, local_sem=S("snd"))
+
+    inc(dv.memset(T.ones[:], 1.0), "on")
+    if isrank:
+        inc(sy.dma_start(T.kvown[:, 0:128], T.k[:, 0:128]), "ld_kv", 16)
+        inc(ac.dma_start(T.kvown[:, 256:384], T.k[:, 128:256]), "ld_kv", 16)
+        inc(sy.dma_start(T.kvown[:, 128:256], T.v[:, 0:128]), "ld_kv", 16)
+        inc(ac.dma_start(T.kvown[:, 384:512], T.v[:, 128:256]), "ld_kv", 16)
+        inc(sy.dma_start(T.qs[:], T.q[:]), "ld_q", 16)
+        need(g, "ld_kv")
+        emit("kvx")
+        need(g, "ld_q")
+        emit("q")
+        emit("kvl")
+    need(g, "on")
+    inc(g.affine_select(T.ident[:], T.ones[:], [[-1, 128]], A.is_equal, 0.0, 0, 1), "id")
+    if "qrel" in calls:
+        need(g, "qr")
+        emit("qrel")
+    need(g, "kd")
+    emit("fwd")
+
+    def kvap(s):
+        if s < 3 and me["ranks"][s] == core:
+            return T.kvown, h * 256
+        return T.kv, s * 256
+
+    def Kap(s):
+        t, o = kvap(s)
+        return t[:, o:o + 128]
+
+    def Vap(s):
+        t, o = kvap(s)
+        return t[:, o + 128:o + 256]
+
+    grp = [[0, 1, 2, 3 + i], [s for s in (3, 4, 5) if s != 3 + i]]
+    Q, qdep, OUT = [], [], []
+    for b, (owner, kind) in enumerate(blocks):
+        if owner == core:
+            Q.append(T.qs[:, h * 128:h * 128 + 128])
+            qdep.append("ld_q")
+            OUT.append((T["oin%d" % h], 0, 128, 129))
+        else:
+            Q.append(T.qin[:, b * 256 + h * 128:b * 256 + h * 128 + 128])
+            qdep.append("qa%d" % b)
+            OUT.append((T["os%d" % b], 0, 128, 129) if kind == "own" else (T["os%d" % b], 2, 0, 1))
+
+    def ncol(b):
+        t, _o, n, _l = OUT[b]
+        return t[:, n:n + 1]
+
+    nm0 = [T.sb[:, b:b + 1] for b in range(2)]
+    nmg = [T.sb[:, 2 + b:3 + b] for b in range(2)]
+    lsum = [[T.sf[:, 2 * k + b:2 * k + b + 1] for k in range(2)] for b in range(2)]
+    aL = [T.sf[:, 4 + b:5 + b] for b in range(2)]
+
+    def nn(s, b, k):
+        return "%s%d%d" % (s, b, k)
+
+    def stS(b, k):
+        need(pe, qdep[b])
+        if k == 0:
+            need(pe, "kl", "kd", "ld_kv")
+        else:
+            need(pe, "kf")
+        for j, s in enumerate(grp[k]):
+            inc(pe.matmul(T[nn("S", b, k)][:, j * 128:(j + 1) * 128], Q[b], Kap(s), start=True, stop=True), nn("sS", b, k))
+
+    def stM(b, k):
+        need(dv, nn("sS", b, k))
+        n = 128 * len(grp[k])
+        inc(dv.tensor_reduce(nm0[b] if k == 0 else nmg[b], T[nn("S", b, k)][:, 0:n], X, A.max, negate=True), nn("sM", b, k))
+
+    def stN(b):
+        need(dv, nn("sM", b, 0), nn("sM", b, 1))
+        inc(dv.tensor_tensor(ncol(b), nmg[b], nm0[b], A.min), "sN%d" % b)
+
+    def stE(b, k):
+        need(ac, nn("sS", b, k), nn("sM", b, k))
+        if k == 1:
+            need(ac, "sN%d" % b)
+        n = 128 * len(grp[k])
+        inc(ac.activation(T[nn("p", b, k)][:, 0:n], T[nn("S", b, k)][:, 0:n], Exp, bias=nm0[b] if k == 0 else ncol(b),
+                          scale=1.0, accum_out=lsum[b][k]), nn("sE", b, k))
+
+    def stAL(b):
+        need(ac, nn("sM", b, 0), "sN%d" % b)
+        inc(ac.activation(aL[b], nm0[b], Exp, bias=ncol(b), scale=-1.0), "sA%d" % b)
+
+    def stT(b, k):
+        need(pe, nn("sE", b, k), "id")
+        for j in range(len(grp[k])):
+            inc(pe.transpose(T["PT%d" % b][:, j * 128:(j + 1) * 128], T[nn("p", b, k)][:, j * 128:(j + 1) * 128], T.ident[:]),
+                nn("sT", b, k))
+
+    def stC(b, k):
+        need(dv, nn("sT", b, k))
+        n = 128 * len(grp[k])
+        inc(dv.tensor_copy(T[nn("pt", b, k)][:, 0:n], T["PT%d" % b][:, 0:n]), nn("sC", b, k))
+
+    def oacc(b, k):
+        return T["O%d" % b][:, 0:128] if k == 0 else T[nn("S", b, 0)][:, 0:128]
+
+    def stPV(b, k):
+        need(pe, nn("sC", b, k))
+        last = len(grp[k]) - 1
+        for j, s in enumerate(grp[k]):
+            inc(pe.matmul(oacc(b, k), T[nn("pt", b, k)][:, j * 128:(j + 1) * 128], Vap(s), start=(j == 0), stop=(j == last)),
+                nn("sO", b, k))
+
+    def stSC(b):
+        need(dv, "sA%d" % b, nn("sO", b, 0))
+        inc(dv.tensor_scalar(T["ol%d" % b][:], oacc(b, 0), aL[b], None, A.mult), "sL%d" % b)
+
+    def stLO(b):
+        need(dv, nn("sE", b, 0), nn("sE", b, 1), "sA%d" % b)
+        t, _o, _n, l = OUT[b]
+        inc(dv.tensor_scalar(t[:, l:l + 1], lsum[b][0], aL[b], lsum[b][1], A.mult, A.add), "sF%d" % b)
+
+    def stF(b):
+        need(dv, "sL%d" % b, nn("sO", b, 1))
+        t, o, _n, _l = OUT[b]
+        inc(dv.tensor_tensor(t[:, o:o + 128], T["ol%d" % b][:], oacc(b, 1), A.add), "sF%d" % b)
+
+    for st in (stS, stM, stE, stT, stC, stPV):
+        for b in (0, 1):
+            st(b, 0)
+    od = [1, 0] if i == 2 else [0, 1]
+    for b in od:
+        stS(b, 1)
+    for b in od:
+        stM(b, 1)
+        stN(b)
+    for b in od:
+        stE(b, 1)
+        stAL(b)
+    for b in od:
+        stSC(b)
+    for b in od:
+        stT(b, 1)
+    for b in od:
+        stC(b, 1)
+        stLO(b)
+    for b in od:
+        stPV(b, 1)
+    for b in od:
+        stF(b)
+    for b in od:
+        if "o%d" % b in calls:
+            need(g, "sN%d" % b, "sF%d" % b)
+            emit("o%d" % b)
+
+    if isrank:
+        lb = [b for b in range(2) if blocks[b][0] == core][0]
+        for k in ([h, 1 - h] if core == me["PR"] else [1 - h, h]):
+            o, c = T["oin%d" % k], "c%d" % k
+            deps = ["oa%d" % k] + (["sN%d" % lb, "sF%d" % lb] if k == h else [])
+            cm, cs, cr = T.sf[:, 8 + k:9 + k], T.sf[:, 10 + k:11 + k], T.sf[:, 12 + k:13 + k]
+            ce, cl, cw = T.sf[:, 16 + 2 * k:18 + 2 * k], T.sf[:, 20 + 2 * k:22 + 2 * k], T.sf[:, 24 + 2 * k:26 + 2 * k]
+            ta, tb = T["ta%d" % k], T["tb%d" % k]
+            need(dv, *deps)
+            inc(dv.tensor_tensor(cm, o[:, 128:129], o[:, 136:137], A.min), c)
+            need(ac, *deps)
+            need(ac, c)
+            inc(ac.activation(ce, o[:, 128:144:8], Exp, bias=cm, scale=-1.0), c)
+            need(dv, c)
+            inc(dv.tensor_tensor(cl, ce, o[:, 129:145:8], A.mult), c)
+            need(dv, c)
+            inc(dv.tensor_reduce(cs, cl, X, A.add), c)
+            need(dv, c)
+            inc(dv.reciprocal(cr, cs), c)
+            need(dv, c)
+            inc(dv.tensor_scalar(cw, ce, cr, None, A.mult), c)
+            need(ac, c)
+            need(dv, c)
+            inc(ac.activation(ta[:], o[:, 0:128], Copy, scale=T.sf[:, 24 + 2 * k:25 + 2 * k]), c)
+            inc(dv.tensor_scalar(tb[:], o[:, 138:266], T.sf[:, 25 + 2 * k:26 + 2 * k], None, A.mult), c)
+            need(dv, c)
+            inc(dv.tensor_tensor(T.ysb[:, k * 128:k * 128 + 128], ta[:], tb[:], A.add), c)
+            need(sy, c)
+            inc(sy.dma_start(T.y[:, k * 128:k * 128 + 128], T.ysb[:, k * 128:k * 128 + 128]), "st", 16)
+
+    for n in sorted(tot):
+        need(g, n)

@@ -3,7 +3,7 @@ from concourse.mybir import AluOpType, AxisListType, ActivationFunctionType
 
 BF, F32 = "bfloat16", "float32"
 SCRATCH = {
-    "kvown": ("sbuf", [128, 512], BF),
+    "kvown": ("sbuf", [128, 2, 256], BF),
     "qs": ("sbuf", [128, 256], BF),
     "kv": ("sbuf", [128, 6 * 256], BF),
     "qin": ("sbuf", [128, 512], BF),
@@ -11,7 +11,7 @@ SCRATCH = {
     "ones": ("sbuf", [128, 128], BF),
     "ident": ("sbuf", [128, 128], BF),
     "sb": ("sbuf", [128, 16], BF),
-    "sf": ("sbuf", [128, 32], F32),
+    "sf": ("sbuf", [128, 48], F32),
     "ysb": ("sbuf", [128, 256], BF),
 }
 for _q in range(2):
@@ -27,11 +27,11 @@ for _q in range(2):
         SCRATCH["pt%d%d" % (_q, _g)] = ("sbuf", [128, 512], BF)
         SCRATCH["S%d%d" % (_q, _g)] = ("psum", [128, 512], F32)
 
-SEMAPHORES = ["ld_kv", "ld_q", "kl", "kd", "kf", "qa0", "qa1", "qr", "oa0", "oa1", "snd", "st", "on", "id", "c0", "c1"]
+SEMAPHORES = ["ld_kv", "ld_q", "kl", "kd", "kf", "qa0", "qa1", "qr", "oa0", "oa1", "snd", "st", "on", "id", "c0", "c1",
+              "e0", "e1"]
 for _q in range(2):
-    SEMAPHORES += ["%s%d" % (s, _q) for s in ("sN", "sA", "sL", "sF")]
     for _g in range(2):
-        SEMAPHORES += ["%s%d%d" % (s, _q, _g) for s in ("sS", "sM", "sE", "sT", "sC", "sO")]
+        SEMAPHORES += ["%s%d%d" % (s, _q, _g) for s in ("sS", "sM", "sE", "sT", "sC", "sO", "sN", "sA", "sL", "sF")]
 
 
 def _bits(m):
@@ -97,8 +97,8 @@ def _sends(c, P, topo):
                              dsts=[(PL["W"][k][r], "kv", (3 + r) * 256, (4 + r) * 256)],
                              sem="kd", eng=lo[k * hl:(k + 1) * hl]) for k in range(2)]
         if c != me["PR"]:
-            calls["q"] = [dict(src=("qs", 0, 256), dsts=[(me["W"][h][1], "qrel", 0, 256)], sem="qr", eng=hi[:hh_]),
-                          dict(src=("qs", 0, 256), dsts=[(me["W"][1 - h][0], "qin", 0, 256)], sem="qa0", eng=hi[hh_:])]
+            calls["kvx"] += [dict(src=("qs", 0, 256), dsts=[(me["W"][h][1], "qrel", 0, 256)], sem="qr", eng=hi[:hh_]),
+                             dict(src=("qs", 0, 256), dsts=[(me["W"][1 - h][0], "qin", 0, 256)], sem="qa0", eng=hi[hh_:])]
         else:
             t = []
             for k in range(2):
@@ -171,48 +171,48 @@ def rank_program(g, core, T, topo):
         trs = []
         for t in calls[name]:
             b, c0, c1 = t["src"]
+            src = T.kvown[:, c0 // 256, :] if b == "kvown" else T[b][:, c0:c1]
             ids, dsts = [], []
             for (dc, db, d0, d1) in t["dsts"]:
                 rid, pid, _se = topo.addr(dc)
                 ids.append(DstId(rid=rid, pnc=pid))
                 dsts.append(T[db][:, d0:d1])
             trs.append(RemoteDMATransfer(dst_ids=ids, dma_engine_mask=sum(1 << e for e in t["eng"]), remote_sem=S(t["sem"]),
-                                         srcs=[T[b][:, c0:c1]], dsts=dsts, alu_op=0))
+                                         srcs=[src], dsts=dsts, alu_op=0))
             tot["snd"] = tot.get("snd", 0) + len(t["eng"])
         g.remote_dma_fused(trs, local_sem=S("snd"))
 
     inc(dv.memset(T.ones[:], 1.0), "on")
     if isrank:
-        inc(sy.dma_start(T.kvown[:, 0:128], T.k[:, 0:128]), "ld_kv", 16)
-        inc(ac.dma_start(T.kvown[:, 256:384], T.k[:, 128:256]), "ld_kv", 16)
-        inc(sy.dma_start(T.kvown[:, 128:256], T.v[:, 0:128]), "ld_kv", 16)
-        inc(ac.dma_start(T.kvown[:, 384:512], T.v[:, 128:256]), "ld_kv", 16)
+        inc(sy.dma_start(T.kvown[:, :, 0:128], T.k[:]), "ld_kv", 16)
+        inc(ac.dma_start(T.kvown[:, :, 128:256], T.v[:]), "ld_kv", 16)
         inc(sy.dma_start(T.qs[:], T.q[:]), "ld_q", 16)
-        need(g, "ld_kv")
-        emit("kvx")
-        need(g, "ld_q")
-        emit("q")
-        emit("kvl")
     need(g, "on")
     inc(g.affine_select(T.ident[:], T.ones[:], [[-1, 128]], A.is_equal, 0.0, 0, 1), "id")
+    if isrank:
+        need(g, "ld_kv")
+        if "q" not in calls:
+            need(g, "ld_q")
+        emit("kvx")
+        if "q" in calls:
+            need(g, "ld_q")
+            emit("q")
+        emit("kvl")
     if "qrel" in calls:
         need(g, "qr")
         emit("qrel")
     need(g, "kd")
     emit("fwd")
 
-    def kvap(s):
-        if s < 3 and me["ranks"][s] == core:
-            return T.kvown, h * 256
-        return T.kv, s * 256
-
     def Kap(s):
-        t, o = kvap(s)
-        return t[:, o:o + 128]
+        if s < 3 and me["ranks"][s] == core:
+            return T.kvown[:, h, 0:128]
+        return T.kv[:, s * 256:s * 256 + 128]
 
     def Vap(s):
-        t, o = kvap(s)
-        return t[:, o + 128:o + 256]
+        if s < 3 and me["ranks"][s] == core:
+            return T.kvown[:, h, 128:256]
+        return T.kv[:, s * 256 + 128:s * 256 + 256]
 
     grp = [[0, 1, 2, 3 + i], [s for s in (3, 4, 5) if s != 3 + i]]
     Q, qdep, OUT = [], [], []
@@ -226,6 +226,9 @@ def rank_program(g, core, T, topo):
             qdep.append("qa%d" % b)
             OUT.append((T["os%d" % b], 0, 128, 129) if kind == "own" else (T["os%d" % b], 2, 0, 1))
 
+    def nn(s, b, k):
+        return "%s%d%d" % (s, b, k)
+
     def ncol(b):
         t, _o, n, _l = OUT[b]
         return t[:, n:n + 1]
@@ -234,9 +237,6 @@ def rank_program(g, core, T, topo):
     nmg = [T.sb[:, 2 + b:3 + b] for b in range(2)]
     lsum = [[T.sf[:, 2 * k + b:2 * k + b + 1] for k in range(2)] for b in range(2)]
     aL = [T.sf[:, 4 + b:5 + b] for b in range(2)]
-
-    def nn(s, b, k):
-        return "%s%d%d" % (s, b, k)
 
     def stS(b, k):
         need(pe, qdep[b])
@@ -254,19 +254,19 @@ def rank_program(g, core, T, topo):
 
     def stN(b):
         need(dv, nn("sM", b, 0), nn("sM", b, 1))
-        inc(dv.tensor_tensor(ncol(b), nmg[b], nm0[b], A.min), "sN%d" % b)
+        inc(dv.tensor_tensor(ncol(b), nmg[b], nm0[b], A.min), nn("sN", b, 1))
 
     def stE(b, k):
         need(ac, nn("sS", b, k), nn("sM", b, k))
         if k == 1:
-            need(ac, "sN%d" % b)
+            need(ac, nn("sN", b, 1))
         n = 128 * len(grp[k])
         inc(ac.activation(T[nn("p", b, k)][:, 0:n], T[nn("S", b, k)][:, 0:n], Exp, bias=nm0[b] if k == 0 else ncol(b),
                           scale=1.0, accum_out=lsum[b][k]), nn("sE", b, k))
 
     def stAL(b):
-        need(ac, nn("sM", b, 0), "sN%d" % b)
-        inc(ac.activation(aL[b], nm0[b], Exp, bias=ncol(b), scale=-1.0), "sA%d" % b)
+        need(ac, nn("sM", b, 0), nn("sN", b, 1))
+        inc(ac.activation(aL[b], nm0[b], Exp, bias=ncol(b), scale=-1.0), nn("sA", b, 1))
 
     def stT(b, k):
         need(pe, nn("sE", b, k), "id")
@@ -290,18 +290,18 @@ def rank_program(g, core, T, topo):
                 nn("sO", b, k))
 
     def stSC(b):
-        need(dv, "sA%d" % b, nn("sO", b, 0))
-        inc(dv.tensor_scalar(T["ol%d" % b][:], oacc(b, 0), aL[b], None, A.mult), "sL%d" % b)
+        need(dv, nn("sA", b, 1), nn("sO", b, 0))
+        inc(dv.tensor_scalar(T["ol%d" % b][:], oacc(b, 0), aL[b], None, A.mult), nn("sL", b, 1))
 
     def stLO(b):
-        need(dv, nn("sE", b, 0), nn("sE", b, 1), "sA%d" % b)
+        need(dv, nn("sE", b, 0), nn("sE", b, 1), nn("sA", b, 1))
         t, _o, _n, l = OUT[b]
-        inc(dv.tensor_scalar(t[:, l:l + 1], lsum[b][0], aL[b], lsum[b][1], A.mult, A.add), "sF%d" % b)
+        inc(dv.tensor_scalar(t[:, l:l + 1], lsum[b][0], aL[b], lsum[b][1], A.mult, A.add), nn("sF", b, 1))
 
     def stF(b):
-        need(dv, "sL%d" % b, nn("sO", b, 1))
+        need(dv, nn("sL", b, 1), nn("sO", b, 1))
         t, o, _n, _l = OUT[b]
-        inc(dv.tensor_tensor(t[:, o:o + 128], T["ol%d" % b][:], oacc(b, 1), A.add), "sF%d" % b)
+        inc(dv.tensor_tensor(t[:, o:o + 128], T["ol%d" % b][:], oacc(b, 1), A.add), nn("sF", b, 1))
 
     for st in (stS, stM, stE, stT, stC, stPV):
         for b in (0, 1):
@@ -328,36 +328,35 @@ def rank_program(g, core, T, topo):
         stF(b)
     for b in od:
         if "o%d" % b in calls:
-            need(g, "sN%d" % b, "sF%d" % b)
+            need(g, nn("sN", b, 1), nn("sF", b, 1))
             emit("o%d" % b)
 
     if isrank:
         lb = [b for b in range(2) if blocks[b][0] == core][0]
         for k in ([h, 1 - h] if core == me["PR"] else [1 - h, h]):
-            o, c = T["oin%d" % k], "c%d" % k
-            deps = ["oa%d" % k] + (["sN%d" % lb, "sF%d" % lb] if k == h else [])
+            o, c, e = T["oin%d" % k], "c%d" % k, "e%d" % k
+            deps = ["oa%d" % k] + ([nn("sN", lb, 1), nn("sF", lb, 1)] if k == h else [])
             cm, cs, cr = T.sf[:, 8 + k:9 + k], T.sf[:, 10 + k:11 + k], T.sf[:, 12 + k:13 + k]
-            ce, cl, cw = T.sf[:, 16 + 2 * k:18 + 2 * k], T.sf[:, 20 + 2 * k:22 + 2 * k], T.sf[:, 24 + 2 * k:26 + 2 * k]
+            ce, cl = T.sf[:, 16 + 2 * k:18 + 2 * k], T.sf[:, 20 + 2 * k:22 + 2 * k]
             ta, tb = T["ta%d" % k], T["tb%d" % k]
             need(dv, *deps)
             inc(dv.tensor_tensor(cm, o[:, 128:129], o[:, 136:137], A.min), c)
             need(ac, *deps)
             need(ac, c)
             inc(ac.activation(ce, o[:, 128:144:8], Exp, bias=cm, scale=-1.0), c)
+            need(ac, c)
             need(dv, c)
+            inc(ac.activation(ta[:], o[:, 0:128], Copy, scale=T.sf[:, 16 + 2 * k:17 + 2 * k]), e)
+            inc(ac.activation(tb[:], o[:, 138:266], Copy, scale=T.sf[:, 17 + 2 * k:18 + 2 * k]), e)
             inc(dv.tensor_tensor(cl, ce, o[:, 129:145:8], A.mult), c)
             need(dv, c)
             inc(dv.tensor_reduce(cs, cl, X, A.add), c)
             need(dv, c)
             inc(dv.reciprocal(cr, cs), c)
+            need(dv, e)
+            inc(dv.tensor_tensor(ta[:], ta[:], tb[:], A.add), c)
             need(dv, c)
-            inc(dv.tensor_scalar(cw, ce, cr, None, A.mult), c)
-            need(ac, c)
-            need(dv, c)
-            inc(ac.activation(ta[:], o[:, 0:128], Copy, scale=T.sf[:, 24 + 2 * k:25 + 2 * k]), c)
-            inc(dv.tensor_scalar(tb[:], o[:, 138:266], T.sf[:, 25 + 2 * k:26 + 2 * k], None, A.mult), c)
-            need(dv, c)
-            inc(dv.tensor_tensor(T.ysb[:, k * 128:k * 128 + 128], ta[:], tb[:], A.add), c)
+            inc(dv.tensor_scalar(T.ysb[:, k * 128:k * 128 + 128], ta[:], cr, None, A.mult), c)
             need(sy, c)
             inc(sy.dma_start(T.y[:, k * 128:k * 128 + 128], T.ysb[:, k * 128:k * 128 + 128]), "st", 16)
 

@@ -2,36 +2,34 @@ from concourse.bass import DstId, RemoteDMATransfer
 from concourse.mybir import AluOpType, AxisListType, ActivationFunctionType
 
 BF, F32 = "bfloat16", "float32"
+KINDS = ["own", "plane", "mate", "diag"]
 SCRATCH = {
     "kvown": ("sbuf", [128, 2, 256], BF),
     "qs": ("sbuf", [128, 256], BF),
-    "kv": ("sbuf", [128, 6 * 256], BF),
-    "qin": ("sbuf", [128, 512], BF),
+    "kv": ("sbuf", [128, 3 * 256], BF),
+    "qin": ("sbuf", [128, 3 * 128], BF),
     "qrel": ("sbuf", [128, 256], BF),
     "ones": ("sbuf", [128, 128], BF),
     "ident": ("sbuf", [128, 128], BF),
-    "sb": ("sbuf", [128, 16], BF),
     "sf": ("sbuf", [128, 48], F32),
     "ysb": ("sbuf", [128, 256], BF),
 }
-for _q in range(2):
-    SCRATCH["os%d" % _q] = ("sbuf", [128, 136], BF)
-    SCRATCH["oin%d" % _q] = ("sbuf", [128, 272], BF)
-    SCRATCH["ol%d" % _q] = ("sbuf", [128, 128], F32)
-    SCRATCH["ta%d" % _q] = ("sbuf", [128, 128], F32)
-    SCRATCH["tb%d" % _q] = ("sbuf", [128, 128], F32)
-    SCRATCH["PT%d" % _q] = ("psum", [128, 1024], BF)
-    SCRATCH["O%d" % _q] = ("psum", [128, 512], F32)
-    for _g in range(2):
-        SCRATCH["p%d%d" % (_q, _g)] = ("sbuf", [128, 512], BF)
-        SCRATCH["pt%d%d" % (_q, _g)] = ("sbuf", [128, 512], BF)
-        SCRATCH["S%d%d" % (_q, _g)] = ("psum", [128, 512], F32)
+for _b in range(3):
+    SCRATCH["os%d" % _b] = ("sbuf", [128, 136], BF)
+    SCRATCH["p%d" % _b] = ("sbuf", [128, 384], BF)
+    SCRATCH["pt%d" % _b] = ("sbuf", [128, 384], BF)
+    SCRATCH["S%d" % _b] = ("psum", [128, 512], F32)
+    SCRATCH["PT%d" % _b] = ("psum", [128, 1024], BF)
+for _k in range(2):
+    SCRATCH["oin%d" % _k] = ("sbuf", [128, 4 * 136], BF)
+    SCRATCH["dg%d" % _k] = ("sbuf", [128, 512], BF)
+    SCRATCH["Y%d" % _k] = ("psum", [128, 512], F32)
 
-SEMAPHORES = ["ld_kv", "ld_q", "kl", "kd", "kf", "qa0", "qa1", "qr", "oa0", "oa1", "snd", "st", "on", "id", "c0", "c1",
-              "e0", "e1"]
-for _q in range(2):
-    for _g in range(2):
-        SEMAPHORES += ["%s%d%d" % (s, _q, _g) for s in ("sS", "sM", "sE", "sT", "sC", "sO", "sN", "sA", "sL", "sF")]
+SEMAPHORES = ["ld_kv", "ld_q", "kl", "qp", "qn0", "qn1", "qx", "oa0", "oa1", "snd", "st", "on", "id"]
+for _b in range(3):
+    SEMAPHORES += ["%s%d" % (s, _b) for s in ("sS", "sM", "sE", "sT", "sC", "sO", "sF")]
+for _k in range(2):
+    SEMAPHORES += ["c%d" % _k, "y%d" % _k] + ["g%d%d" % (_k, i) for i in range(4)]
 
 
 def _bits(m):
@@ -46,17 +44,22 @@ def _plan(T, topo):
         ranks = [c for c in cores if topo.chip(c) == X]
         mate = [Y for Y in chips if topo.mates(X, Y)][0]
         plane = [Y for Y in chips if topo.same_plane(X, Y)][0]
+        diag = [Y for Y in chips if topo.mates(plane, Y)][0]
         probe = [c for c in cores if topo.chip(c) == mate][0]
-        owners = [c for c in range(topo.CHIPS * topo.CORES_PER_CHIP) if topo.chip(c) == X and topo.may_write(c, probe)]
+        onchip = [c for c in range(topo.CHIPS * topo.CORES_PER_CHIP) if topo.chip(c) == X]
+        owners = [c for c in onchip if topo.may_write(c, probe)]
         NP = [r for r in ranks if r not in owners]
         PR = [r for r in ranks if r in owners][0]
-        W = []
+        W, relay = [], []
         for h in range(2):
-            od = [c for c in owners if topo.die(c) == topo.die(NP[h])]
-            B = PR if PR in od else od[-1]
-            A = [c for c in od if c != B][0]
-            W.append([NP[h], A, B])
-        P[X] = dict(ranks=ranks, mate=mate, plane=plane, NP=NP, PR=PR, W=W)
+            dd = topo.die(NP[h])
+            od = [c for c in owners if topo.die(c) == dd]
+            nd = [c for c in onchip if topo.die(c) == dd and c not in owners and c != NP[h]]
+            free = [c for c in od if c != PR]
+            mt, dg = (PR, free[0]) if PR in od else (free[0], free[1])
+            W.append({"own": NP[h], "plane": nd[0], "mate": mt, "diag": dg})
+            relay.append([(free[0], ["mate"]), (free[1], ["diag"])] if len(free) > 1 else [(free[0], ["diag", "mate"])])
+        P[X] = dict(chip=X, own=X, ranks=ranks, mate=mate, plane=plane, diag=diag, NP=NP, PR=PR, W=W, relay=relay)
     return P
 
 
@@ -65,67 +68,73 @@ def _role(c, P, topo):
     if X not in P:
         return None
     for h in range(2):
-        for i, w in enumerate(P[X]["W"][h]):
-            if w == c:
-                return (h, i)
+        for kind in KINDS:
+            if P[X]["W"][h][kind] == c:
+                return (h, kind)
     return None
 
 
 def _blocks(c, P, topo):
     me = P[topo.chip(c)]
-    M = P[me["mate"]]
-    h, i = _role(c, P, topo)
-    if i == 0:
-        return [(me["NP"][1 - h], "own"), (me["NP"][h], "own")]
-    if i == 1:
-        return [(M["PR"], "mate"), (M["NP"][h], "mate")]
-    return [(me["PR"], "own"), (M["NP"][1 - h], "mate")]
+    h, kind = _role(c, P, topo)
+    S = P[me[kind]]
+    if kind == "own":
+        return [(S["PR"], "qp"), (S["NP"][1 - h], "qx"), (S["NP"][h], "ld_q")]
+    if kind == "plane":
+        return [(S["NP"][0], "qn0"), (S["NP"][1], "qn1"), (S["PR"], "qp")]
+    return [(S["PR"], "qp"), (S["NP"][0], "qn0"), (S["NP"][1], "qn1")]
+
+
+def _qdst(w, owner, P, topo):
+    b = [o for o, _s in _blocks(w, P, topo)].index(owner)
+    return (w, "qin", b * 128, b * 128 + 128)
 
 
 def _sends(c, P, topo):
     me = P[topo.chip(c)]
-    M, PL = P[me["mate"]], P[me["plane"]]
-    h, i = _role(c, P, topo)
-    lo = _bits(topo.mask(c, M["ranks"][0]))
-    on = _bits(topo.mask(c, [w for w in me["W"][0] + me["W"][1] if w != c][0]))
+    M, PL, D = P[me["mate"]], P[me["plane"]], P[me["diag"]]
+    far = {"mate": M, "diag": D}
+    h, kind = _role(c, P, topo)
+    lo = _bits(topo.mask(c, PL["ranks"][0]))
+    on = _bits(topo.mask(c, [w for w in me["W"][0].values() if w != c][0]))
     hi = [e for e in on if e not in lo]
-    hl, hh_ = len(lo) // 2, len(hi) // 2
+    hl, hh = len(lo) // 2, len(hi) // 2
     calls = {}
     if c in me["ranks"]:
         r = me["ranks"].index(c)
-        calls["kvx"] = [dict(src=("kvown", k * 256, k * 256 + 256),
-                             dsts=[(PL["W"][k][r], "kv", (3 + r) * 256, (4 + r) * 256)],
-                             sem="kd", eng=lo[k * hl:(k + 1) * hl]) for k in range(2)]
-        if c != me["PR"]:
-            calls["kvx"] += [dict(src=("qs", 0, 256), dsts=[(me["W"][h][1], "qrel", 0, 256)], sem="qr", eng=hi[:hh_]),
-                             dict(src=("qs", 0, 256), dsts=[(me["W"][1 - h][0], "qin", 0, 256)], sem="qa0", eng=hi[hh_:])]
-        else:
-            t = []
-            for k in range(2):
-                t.append(dict(src=("qs", k * 128, k * 128 + 128), dsts=[(M["W"][k][1], "qin", k * 128, k * 128 + 128)],
-                              sem="qa0", eng=lo[k * hl:(k + 1) * hl]))
-                if me["W"][k][2] != c:
-                    t.append(dict(src=("qs", k * 128, k * 128 + 128),
-                                  dsts=[(me["W"][k][2], "qin", k * 128, k * 128 + 128)], sem="qa0", eng=hi))
-            calls["q"] = t
         t = []
         for k in range(2):
-            d = [w for w in me["W"][k] if w != c]
+            src = ("qs", k * 128, k * 128 + 128)
+            if c == me["PR"]:
+                t.append(dict(src=src, dsts=[_qdst(w, c, P, topo) for w in
+                                             (M["W"][k]["mate"], D["W"][k]["diag"], PL["W"][k]["plane"])],
+                              sem="qp", eng=lo[k * hl:(k + 1) * hl]))
+                t.append(dict(src=src, dsts=[_qdst(me["W"][k]["own"], c, P, topo)], sem="qp", eng=hi[k * hh:(k + 1) * hh]))
+            else:
+                d = [(rc, "qrel", k * 128, k * 128 + 128) for rc, _j in me["relay"][h]]
+                if k != h:
+                    d.append(_qdst(me["W"][k]["own"], c, P, topo))
+                t.append(dict(src=src, dsts=d, sem="qx", eng=hi[k * hh:(k + 1) * hh]))
+                t.append(dict(src=src, dsts=[_qdst(PL["W"][k]["plane"], c, P, topo)], sem="qn%d" % h,
+                              eng=lo[k * hl:(k + 1) * hl]))
+        calls["q"] = t
+        t = []
+        for k in range(2):
+            d = [me["W"][k][x] for x in KINDS if me["W"][k][x] != c]
             t.append(dict(src=("kvown", k * 256, k * 256 + 256), dsts=[(w, "kv", r * 256, (r + 1) * 256) for w in d],
-                          sem="kl", eng=hi if len(d) == 3 else lo))
-        calls["kvl"] = t
-    if i == 1:
-        calls["qrel"] = [dict(src=("qrel", k * 128, k * 128 + 128),
-                              dsts=[(M["W"][k][1] if k == h else M["W"][k][2], "qin", 256 + k * 128, 384 + k * 128)],
-                              sem="qa1", eng=lo[k * hl:(k + 1) * hl]) for k in range(2)]
-    others = [w for w in me["W"][h] if w != c]
-    calls["fwd"] = [dict(src=("kv", (3 + i) * 256, (4 + i) * 256), dsts=[(others[k], "kv", (3 + i) * 256, (4 + i) * 256)],
-                         sem="kf", eng=(lo, hi)[k]) for k in range(2)]
-    for b, (owner, kind) in enumerate(_blocks(c, P, topo)):
+                          sem="kl", eng=lo if len(d) == 3 else hi))
+        calls["kv"] = t
+    for j in range(2):
+        for rc, jobs in me["relay"][j]:
+            if rc == c:
+                calls["qrel"] = [dict(src=("qrel", k * 128, k * 128 + 128),
+                                      dsts=[_qdst(far[x]["W"][k][x], me["NP"][j], P, topo) for x in jobs],
+                                      sem="qn%d" % j, eng=lo[k * hl:(k + 1) * hl]) for k in range(2)]
+    off = KINDS.index(kind) * 136
+    for b, (owner, _s) in enumerate(_blocks(c, P, topo)):
         if owner != c:
-            off = 0 if kind == "own" else 136
             calls["o%d" % b] = [dict(src=("os%d" % b, 0, 130), dsts=[(owner, "oin%d" % h, off, off + 130)],
-                                     sem="oa%d" % h, eng=(lo + hi) if topo.chip(owner) == topo.chip(c) else lo)]
+                                     sem="oa%d" % h, eng=_bits(topo.mask(c, owner)))]
     return calls
 
 
@@ -134,7 +143,7 @@ def rank_program(g, core, T, topo):
     role = _role(core, P, topo)
     if role is None:
         return
-    h, i = role
+    h, kind = role
     me = P[topo.chip(core)]
     isrank = core in me["ranks"]
     blocks = _blocks(core, P, topo)
@@ -146,7 +155,7 @@ def rank_program(g, core, T, topo):
     tot = {}
     for Y in P:
         for k in range(2):
-            for w in P[Y]["W"][k]:
+            for w in P[Y]["W"][k].values():
                 if w == core:
                     continue
                 for trs in _sends(w, P, topo).values():
@@ -184,179 +193,135 @@ def rank_program(g, core, T, topo):
 
     inc(dv.memset(T.ones[:], 1.0), "on")
     if isrank:
-        inc(sy.dma_start(T.kvown[:, :, 0:128], T.k[:]), "ld_kv", 16)
-        inc(ac.dma_start(T.kvown[:, :, 128:256], T.v[:]), "ld_kv", 16)
         inc(sy.dma_start(T.qs[:], T.q[:]), "ld_q", 16)
+        inc(ac.dma_start(T.kvown[:, :, 0:128], T.k[:]), "ld_kv", 16)
+        inc(sy.dma_start(T.kvown[:, :, 128:256], T.v[:]), "ld_kv", 16)
     need(g, "on")
     inc(g.affine_select(T.ident[:], T.ones[:], [[-1, 128]], A.is_equal, 0.0, 0, 1), "id")
     if isrank:
+        need(g, "ld_q")
+        emit("q")
         need(g, "ld_kv")
-        if "q" not in calls:
-            need(g, "ld_q")
-        emit("kvx")
-        if "q" in calls:
-            need(g, "ld_q")
-            emit("q")
-        emit("kvl")
+        emit("kv")
     if "qrel" in calls:
-        need(g, "qr")
+        need(g, "qx")
         emit("qrel")
-    need(g, "kd")
-    emit("fwd")
 
     def Kap(s):
-        if s < 3 and me["ranks"][s] == core:
-            return T.kvown[:, h, 0:128]
-        return T.kv[:, s * 256:s * 256 + 128]
+        return T.kvown[:, h, 0:128] if me["ranks"][s] == core else T.kv[:, s * 256:s * 256 + 128]
 
     def Vap(s):
-        if s < 3 and me["ranks"][s] == core:
-            return T.kvown[:, h, 128:256]
-        return T.kv[:, s * 256 + 128:s * 256 + 256]
+        return T.kvown[:, h, 128:256] if me["ranks"][s] == core else T.kv[:, s * 256 + 128:s * 256 + 256]
 
-    grp = [[0, 1, 2, 3 + i], [s for s in (3, 4, 5) if s != 3 + i]]
-    Q, qdep, OUT = [], [], []
-    for b, (owner, kind) in enumerate(blocks):
+    Q, OUT = [], []
+    for b, (owner, _s) in enumerate(blocks):
         if owner == core:
             Q.append(T.qs[:, h * 128:h * 128 + 128])
-            qdep.append("ld_q")
-            OUT.append((T["oin%d" % h], 0, 128, 129))
+            OUT.append(T["oin%d" % h])
         else:
-            Q.append(T.qin[:, b * 256 + h * 128:b * 256 + h * 128 + 128])
-            qdep.append("qa%d" % b)
-            OUT.append((T["os%d" % b], 0, 128, 129) if kind == "own" else (T["os%d" % b], 2, 0, 1))
+            Q.append(T.qin[:, b * 128:b * 128 + 128])
+            OUT.append(T["os%d" % b])
+    lsum = [T.sf[:, b:b + 1] for b in range(3)]
 
-    def nn(s, b, k):
-        return "%s%d%d" % (s, b, k)
+    def nn(s, b):
+        return "%s%d" % (s, b)
 
-    def ncol(b):
-        t, _o, n, _l = OUT[b]
-        return t[:, n:n + 1]
+    def stS(b):
+        need(pe, blocks[b][1], "kl", "ld_kv")
+        for j in range(3):
+            inc(pe.matmul(T[nn("S", b)][:, j * 128:(j + 1) * 128], Q[b], Kap(j), start=True, stop=True), nn("sS", b))
 
-    nm0 = [T.sb[:, b:b + 1] for b in range(2)]
-    nmg = [T.sb[:, 2 + b:3 + b] for b in range(2)]
-    lsum = [[T.sf[:, 2 * k + b:2 * k + b + 1] for k in range(2)] for b in range(2)]
-    aL = [T.sf[:, 4 + b:5 + b] for b in range(2)]
+    def stM(b):
+        need(dv, nn("sS", b))
+        inc(dv.tensor_reduce(OUT[b][:, 128:129], T[nn("S", b)][:, 0:384], X, A.max, negate=True), nn("sM", b))
 
-    def stS(b, k):
-        need(pe, qdep[b])
-        if k == 0:
-            need(pe, "kl", "kd", "ld_kv")
-        else:
-            need(pe, "kf")
-        for j, s in enumerate(grp[k]):
-            inc(pe.matmul(T[nn("S", b, k)][:, j * 128:(j + 1) * 128], Q[b], Kap(s), start=True, stop=True), nn("sS", b, k))
+    def stE(b):
+        need(ac, nn("sS", b), nn("sM", b))
+        inc(ac.activation(T[nn("p", b)][:], T[nn("S", b)][:, 0:384], Exp, bias=OUT[b][:, 128:129], scale=1.0,
+                          accum_out=lsum[b]), nn("sE", b))
 
-    def stM(b, k):
-        need(dv, nn("sS", b, k))
-        n = 128 * len(grp[k])
-        inc(dv.tensor_reduce(nm0[b] if k == 0 else nmg[b], T[nn("S", b, k)][:, 0:n], X, A.max, negate=True), nn("sM", b, k))
+    def stT(b):
+        need(pe, nn("sE", b), "id")
+        for j in range(3):
+            inc(pe.transpose(T[nn("PT", b)][:, j * 128:(j + 1) * 128], T[nn("p", b)][:, j * 128:(j + 1) * 128], T.ident[:]),
+                nn("sT", b))
 
-    def stN(b):
-        need(dv, nn("sM", b, 0), nn("sM", b, 1))
-        inc(dv.tensor_tensor(ncol(b), nmg[b], nm0[b], A.min), nn("sN", b, 1))
+    def stC(b):
+        need(dv, nn("sT", b))
+        inc(dv.tensor_copy(T[nn("pt", b)][:], T[nn("PT", b)][:, 0:384]), nn("sC", b))
 
-    def stE(b, k):
-        need(ac, nn("sS", b, k), nn("sM", b, k))
-        if k == 1:
-            need(ac, nn("sN", b, 1))
-        n = 128 * len(grp[k])
-        inc(ac.activation(T[nn("p", b, k)][:, 0:n], T[nn("S", b, k)][:, 0:n], Exp, bias=nm0[b] if k == 0 else ncol(b),
-                          scale=1.0, accum_out=lsum[b][k]), nn("sE", b, k))
+    def stL(b):
+        need(dv, nn("sE", b))
+        inc(dv.tensor_copy(OUT[b][:, 129:130], lsum[b]), nn("sF", b))
 
-    def stAL(b):
-        need(ac, nn("sM", b, 0), nn("sN", b, 1))
-        inc(ac.activation(aL[b], nm0[b], Exp, bias=ncol(b), scale=-1.0), nn("sA", b, 1))
-
-    def stT(b, k):
-        need(pe, nn("sE", b, k), "id")
-        for j in range(len(grp[k])):
-            inc(pe.transpose(T["PT%d" % b][:, j * 128:(j + 1) * 128], T[nn("p", b, k)][:, j * 128:(j + 1) * 128], T.ident[:]),
-                nn("sT", b, k))
-
-    def stC(b, k):
-        need(dv, nn("sT", b, k))
-        n = 128 * len(grp[k])
-        inc(dv.tensor_copy(T[nn("pt", b, k)][:, 0:n], T["PT%d" % b][:, 0:n]), nn("sC", b, k))
-
-    def oacc(b, k):
-        return T["O%d" % b][:, 0:128] if k == 0 else T[nn("S", b, 0)][:, 0:128]
-
-    def stPV(b, k):
-        need(pe, nn("sC", b, k))
-        last = len(grp[k]) - 1
-        for j, s in enumerate(grp[k]):
-            inc(pe.matmul(oacc(b, k), T[nn("pt", b, k)][:, j * 128:(j + 1) * 128], Vap(s), start=(j == 0), stop=(j == last)),
-                nn("sO", b, k))
-
-    def stSC(b):
-        need(dv, nn("sA", b, 1), nn("sO", b, 0))
-        inc(dv.tensor_scalar(T["ol%d" % b][:], oacc(b, 0), aL[b], None, A.mult), nn("sL", b, 1))
-
-    def stLO(b):
-        need(dv, nn("sE", b, 0), nn("sE", b, 1), nn("sA", b, 1))
-        t, _o, _n, l = OUT[b]
-        inc(dv.tensor_scalar(t[:, l:l + 1], lsum[b][0], aL[b], lsum[b][1], A.mult, A.add), nn("sF", b, 1))
+    def stPV(b):
+        need(pe, nn("sC", b))
+        for j in range(3):
+            inc(pe.matmul(T[nn("S", b)][:, 0:128], T[nn("pt", b)][:, j * 128:(j + 1) * 128], Vap(j), start=(j == 0),
+                          stop=(j == 2)), nn("sO", b))
 
     def stF(b):
-        need(dv, nn("sL", b, 1), nn("sO", b, 1))
-        t, o, _n, _l = OUT[b]
-        inc(dv.tensor_tensor(t[:, o:o + 128], T["ol%d" % b][:], oacc(b, 1), A.add), nn("sF", b, 1))
+        need(ac, nn("sO", b))
+        inc(ac.activation(OUT[b][:, 0:128], T[nn("S", b)][:, 0:128], Copy), nn("sF", b))
 
-    for st in (stS, stM, stE, stT, stC, stPV):
-        for b in (0, 1):
-            st(b, 0)
-    od = [1, 0] if i == 2 else [0, 1]
-    for b in od:
-        stS(b, 1)
-    for b in od:
-        stM(b, 1)
-        stN(b)
-    for b in od:
-        stE(b, 1)
-        stAL(b)
-    for b in od:
-        stSC(b)
-    for b in od:
-        stT(b, 1)
-    for b in od:
-        stC(b, 1)
-        stLO(b)
-    for b in od:
-        stPV(b, 1)
-    for b in od:
+    for st in (stS, stM, stE):
+        for b in range(3):
+            st(b)
+    stT(0)
+    stT(1)
+    stC(0)
+    stL(0)
+    stC(1)
+    stL(1)
+    stPV(0)
+    stT(2)
+    stC(2)
+    stL(2)
+    stPV(1)
+    stPV(2)
+    for b in range(3):
         stF(b)
-    for b in od:
+    for b in range(3):
         if "o%d" % b in calls:
-            need(g, nn("sN", b, 1), nn("sF", b, 1))
+            need(g, nn("sM", b), nn("sF", b))
             emit("o%d" % b)
 
     if isrank:
-        lb = [b for b in range(2) if blocks[b][0] == core][0]
-        for k in ([h, 1 - h] if core == me["PR"] else [1 - h, h]):
-            o, c, e = T["oin%d" % k], "c%d" % k, "e%d" % k
-            deps = ["oa%d" % k] + ([nn("sN", lb, 1), nn("sF", lb, 1)] if k == h else [])
+        need(dv, "id")
+        need(ac, "id")
+        for k in range(2):
+            o, c, dg, Yk = T["oin%d" % k], "c%d" % k, T["dg%d" % k], T["Y%d" % k]
+            deps = ["oa%d" % k]
+            for b, (owner, _s) in enumerate(blocks):
+                if owner == core and k == h:
+                    deps += [nn("sM", b), nn("sF", b)]
             cm, cs, cr = T.sf[:, 8 + k:9 + k], T.sf[:, 10 + k:11 + k], T.sf[:, 12 + k:13 + k]
-            ce, cl = T.sf[:, 16 + 2 * k:18 + 2 * k], T.sf[:, 20 + 2 * k:22 + 2 * k]
-            ta, tb = T["ta%d" % k], T["tb%d" % k]
+            ce, cl = T.sf[:, 16 + 4 * k:20 + 4 * k], T.sf[:, 24 + 4 * k:28 + 4 * k]
+            nm4, l4 = o[:, 128:537:136], o[:, 129:538:136]
             need(dv, *deps)
-            inc(dv.tensor_tensor(cm, o[:, 128:129], o[:, 136:137], A.min), c)
+            inc(dv.tensor_reduce(cm, nm4, X, A.min), c)
             need(ac, *deps)
             need(ac, c)
-            inc(ac.activation(ce, o[:, 128:144:8], Exp, bias=cm, scale=-1.0), c)
+            inc(ac.activation(ce, nm4, Exp, bias=cm, scale=-1.0), c)
             need(ac, c)
             need(dv, c)
-            inc(ac.activation(ta[:], o[:, 0:128], Copy, scale=T.sf[:, 16 + 2 * k:17 + 2 * k]), e)
-            inc(ac.activation(tb[:], o[:, 138:266], Copy, scale=T.sf[:, 17 + 2 * k:18 + 2 * k]), e)
-            inc(dv.tensor_tensor(cl, ce, o[:, 129:145:8], A.mult), c)
+            need(pe, *deps)
+            for n, i in enumerate((2, 0, 3, 1)):
+                col = T.sf[:, 16 + 4 * k + i:17 + 4 * k + i]
+                d = dg[:, i * 128:(i + 1) * 128]
+                if i >= 2:
+                    inc(dv.tensor_scalar(d, T.ident[:], col, None, A.mult), "g%d%d" % (k, i))
+                else:
+                    inc(ac.activation(d, T.ident[:], Copy, scale=col), "g%d%d" % (k, i))
+                need(pe, "g%d%d" % (k, i))
+                inc(pe.matmul(Yk[:, 0:128], d, o[:, i * 136:i * 136 + 128], start=(n == 0), stop=(n == 3)), "y%d" % k)
+            inc(dv.tensor_tensor(cl, ce, l4, A.mult), c)
             need(dv, c)
             inc(dv.tensor_reduce(cs, cl, X, A.add), c)
             need(dv, c)
             inc(dv.reciprocal(cr, cs), c)
-            need(dv, e)
-            inc(dv.tensor_tensor(ta[:], ta[:], tb[:], A.add), c)
-            need(dv, c)
-            inc(dv.tensor_scalar(T.ysb[:, k * 128:k * 128 + 128], ta[:], cr, None, A.mult), c)
+            need(dv, c, "y%d" % k)
+            inc(dv.tensor_scalar(T.ysb[:, k * 128:k * 128 + 128], Yk[:, 0:128], cr, None, A.mult), c)
             need(sy, c)
             inc(sy.dma_start(T.y[:, k * 128:k * 128 + 128], T.ysb[:, k * 128:k * 128 + 128]), "st", 16)
 

@@ -9,7 +9,8 @@ SCRATCH = {
     "kv": ("sbuf", [128, 3 * 256], BF),
     "qin": ("sbuf", [128, 3 * 128], BF),
     "qrel": ("sbuf", [128, 256], BF),
-    "ones": ("sbuf", [128, 128], BF),
+    "dif": ("sbuf", [128, 128], BF),
+    "sq": ("sbuf", [128, 128], BF),
     "ident": ("sbuf", [128, 128], BF),
     "sf": ("sbuf", [128, 48], F32),
     "ysb": ("sbuf", [128, 256], BF),
@@ -25,7 +26,7 @@ for _k in range(2):
     SCRATCH["dg%d" % _k] = ("sbuf", [128, 512], BF)
     SCRATCH["Y%d" % _k] = ("psum", [128, 512], F32)
 
-SEMAPHORES = ["ld_kv", "ld_q", "kl", "qp", "qn0", "qn1", "qx", "oa0", "oa1", "snd", "st", "on", "id"]
+SEMAPHORES = ["ld_kv", "ld_q", "kl", "qp", "qn0", "qn1", "qx", "oa0", "oa1", "snd", "st", "on", "sq", "id"]
 for _b in range(3):
     SEMAPHORES += ["%s%d" % (s, _b) for s in ("sS", "sM", "sE", "sT", "sC", "sO", "sF")]
 for _k in range(2):
@@ -111,12 +112,12 @@ def _sends(c, P, topo):
                               sem="qp", eng=lo[k * hl:(k + 1) * hl]))
                 t.append(dict(src=src, dsts=[_qdst(me["W"][k]["own"], c, P, topo)], sem="qp", eng=hi[k * hh:(k + 1) * hh]))
             else:
-                d = [(rc, "qrel", k * 128, k * 128 + 128) for rc, _j in me["relay"][h]]
                 if k != h:
-                    d.append(_qdst(me["W"][k]["own"], c, P, topo))
-                t.append(dict(src=src, dsts=d, sem="qx", eng=hi[k * hh:(k + 1) * hh]))
+                    t.append(dict(src=src, dsts=[_qdst(me["W"][k]["own"], c, P, topo)], sem="qx", eng=hi))
                 t.append(dict(src=src, dsts=[_qdst(PL["W"][k]["plane"], c, P, topo)], sem="qn%d" % h,
                               eng=lo[k * hl:(k + 1) * hl]))
+        if c != me["PR"]:
+            calls["qr"] = [dict(src=("qs", 0, 256), dsts=[(rc, "qrel", 0, 256) for rc, _j in me["relay"][h]], sem="qx", eng=hi)]
         calls["q"] = t
         t = []
         for k in range(2):
@@ -191,15 +192,19 @@ def rank_program(g, core, T, topo):
             tot["snd"] = tot.get("snd", 0) + len(t["eng"])
         g.remote_dma_fused(trs, local_sem=S("snd"))
 
-    inc(dv.memset(T.ones[:], 1.0), "on")
     if isrank:
         inc(sy.dma_start(T.qs[:], T.q[:]), "ld_q", 16)
         inc(ac.dma_start(T.kvown[:, :, 0:128], T.k[:]), "ld_kv", 16)
         inc(sy.dma_start(T.kvown[:, :, 128:256], T.v[:]), "ld_kv", 16)
-    need(g, "on")
-    inc(g.affine_select(T.ident[:], T.ones[:], [[-1, 128]], A.is_equal, 0.0, 0, 1), "id")
+    inc(g.iota(T.dif[:], [[-1, 128]], 0, 1, allow_small_or_imprecise_dtypes=True), "on")
+    need(dv, "on")
+    inc(dv.tensor_tensor(T.sq[:], T.dif[:], T.dif[:], A.mult), "sq")
+    need(ac, "sq")
+    inc(ac.activation(T.ident[:], T.sq[:], Exp, scale=-100.0), "id")
     if isrank:
         need(g, "ld_q")
+        if "qr" in calls:
+            emit("qr")
         emit("q")
         need(g, "ld_kv")
         emit("kv")

@@ -13,24 +13,26 @@ SCRATCH = {
     "sq": ("sbuf", [128, 128], BF),
     "ident": ("sbuf", [128, 128], BF),
     "sf": ("sbuf", [128, 48], F32),
+    "ss": ("sbuf", [128, 12], F32),
+    "st": ("sbuf", [128, 32], F32),
     "ysb": ("sbuf", [128, 256], BF),
 }
 for _b in range(3):
-    SCRATCH["os%d" % _b] = ("sbuf", [128, 136], BF)
+    SCRATCH["os%d" % _b] = ("sbuf", [128, 128], BF)
     SCRATCH["p%d" % _b] = ("sbuf", [128, 384], BF)
     SCRATCH["pt%d" % _b] = ("sbuf", [128, 384], BF)
     SCRATCH["S%d" % _b] = ("psum", [128, 512], F32)
     SCRATCH["PT%d" % _b] = ("psum", [128, 1024], BF)
 for _k in range(2):
-    SCRATCH["oin%d" % _k] = ("sbuf", [128, 4 * 136], BF)
+    SCRATCH["oin%d" % _k] = ("sbuf", [128, 4 * 128], BF)
     SCRATCH["dg%d" % _k] = ("sbuf", [128, 512], BF)
     SCRATCH["Y%d" % _k] = ("psum", [128, 512], F32)
 
-SEMAPHORES = ["ld_kv", "ld_q", "kl", "qp", "qn0", "qn1", "qx", "oa0", "oa1", "snd", "st", "on", "sq", "id"]
+SEMAPHORES = ["ld_kv", "ld_q", "kl", "qp", "qn0", "qn1", "qx", "sa0", "sa1", "snd", "st", "on", "sq", "id", "fin"]
 for _b in range(3):
     SEMAPHORES += ["%s%d" % (s, _b) for s in ("sS", "sM", "sE", "sT", "sC", "sO", "sF")]
 for _k in range(2):
-    SEMAPHORES += ["c%d" % _k, "y%d" % _k] + ["g%d%d" % (_k, i) for i in range(4)]
+    SEMAPHORES += ["c%d" % _k, "y%d" % _k] + ["g%d%d" % (_k, i) for i in range(4)] + ["oa%d%d" % (_k, i) for i in range(4)]
 
 
 def _bits(m):
@@ -131,11 +133,21 @@ def _sends(c, P, topo):
                 calls["qrel"] = [dict(src=("qrel", k * 128, k * 128 + 128),
                                       dsts=[_qdst(far[x]["W"][k][x], me["NP"][j], P, topo) for x in jobs],
                                       sem="qn%d" % j, eng=lo[k * hl:(k + 1) * hl]) for k in range(2)]
-    off = KINDS.index(kind) * 136
-    for b, (owner, _s) in enumerate(_blocks(c, P, topo)):
-        if owner != c:
-            calls["o%d" % b] = [dict(src=("os%d" % b, 0, 130), dsts=[(owner, "oin%d" % h, off, off + 130)],
-                                     sem="oa%d" % h, eng=_bits(topo.mask(c, owner)))]
+    slot = KINDS.index(kind)
+    rem = [(b, o) for b, (o, _s) in enumerate(_blocks(c, P, topo)) if o != c]
+    for gi, grp in enumerate(([x for x in rem if x[0] == 0], [x for x in rem if x[0] > 0])):
+        t = []
+        for n, (b, o) in enumerate(grp):
+            e = _bits(topo.mask(c, o))
+            w = len(e) // len(grp)
+            cc = 4 * (4 * h + slot)
+            t.append(dict(src=("ss", 4 * b, 4 * b + 2), dsts=[(o, "st", cc, cc + 2)], sem="sa%d" % h,
+                          eng=e[n * w:(n + 1) * w], blk=b))
+        if t:
+            calls["s%d" % gi] = t
+    for b, owner in rem:
+        calls["o%d" % b] = [dict(src=("os%d" % b, 0, 128), dsts=[(owner, "oin%d" % h, slot * 128, slot * 128 + 128)],
+                                 sem="oa%d%d" % (h, slot), eng=_bits(topo.mask(c, owner)))]
     return calls
 
 
@@ -218,15 +230,20 @@ def rank_program(g, core, T, topo):
     def Vap(s):
         return T.kvown[:, h, 128:256] if me["ranks"][s] == core else T.kv[:, s * 256 + 128:s * 256 + 256]
 
-    Q, OUT = [], []
+    slot = KINDS.index(kind)
+    Q, OUT, NM, LS = [], [], [], []
     for b, (owner, _s) in enumerate(blocks):
         if owner == core:
+            cc = 4 * (4 * h + slot)
             Q.append(T.qs[:, h * 128:h * 128 + 128])
-            OUT.append(T["oin%d" % h])
+            OUT.append(T["oin%d" % h][:, slot * 128:slot * 128 + 128])
+            NM.append(T.st[:, cc:cc + 1])
+            LS.append(T.st[:, cc + 1:cc + 2])
         else:
             Q.append(T.qin[:, b * 128:b * 128 + 128])
-            OUT.append(T["os%d" % b])
-    lsum = [T.sf[:, b:b + 1] for b in range(3)]
+            OUT.append(T["os%d" % b][:])
+            NM.append(T.ss[:, 4 * b:4 * b + 1])
+            LS.append(T.ss[:, 4 * b + 1:4 * b + 2])
 
     def nn(s, b):
         return "%s%d" % (s, b)
@@ -238,12 +255,12 @@ def rank_program(g, core, T, topo):
 
     def stM(b):
         need(dv, nn("sS", b))
-        inc(dv.tensor_reduce(OUT[b][:, 128:129], T[nn("S", b)][:, 0:384], X, A.max, negate=True), nn("sM", b))
+        inc(dv.tensor_reduce(NM[b], T[nn("S", b)][:, 0:384], X, A.max, negate=True), nn("sM", b))
 
     def stE(b):
         need(ac, nn("sS", b), nn("sM", b))
-        inc(ac.activation(T[nn("p", b)][:], T[nn("S", b)][:, 0:384], Exp, bias=OUT[b][:, 128:129], scale=1.0,
-                          accum_out=lsum[b]), nn("sE", b))
+        inc(ac.activation(T[nn("p", b)][:], T[nn("S", b)][:, 0:384], Exp, bias=NM[b], scale=1.0,
+                          accum_out=LS[b]), nn("sE", b))
 
     def stT(b):
         need(pe, nn("sE", b), "id")
@@ -255,10 +272,6 @@ def rank_program(g, core, T, topo):
         need(dv, nn("sT", b))
         inc(dv.tensor_copy(T[nn("pt", b)][:], T[nn("PT", b)][:, 0:384]), nn("sC", b))
 
-    def stL(b):
-        need(dv, nn("sE", b))
-        inc(dv.tensor_copy(OUT[b][:, 129:130], lsum[b]), nn("sF", b))
-
     def stPV(b):
         need(pe, nn("sC", b))
         for j in range(3):
@@ -267,7 +280,7 @@ def rank_program(g, core, T, topo):
 
     def stF(b):
         need(ac, nn("sO", b))
-        inc(ac.activation(OUT[b][:, 0:128], T[nn("S", b)][:, 0:128], Copy), nn("sF", b))
+        inc(ac.activation(OUT[b], T[nn("S", b)][:, 0:128], Copy), nn("sF", b))
 
     for st in (stS, stM, stE):
         for b in range(3):
@@ -275,60 +288,75 @@ def rank_program(g, core, T, topo):
     stT(0)
     stT(1)
     stC(0)
-    stL(0)
     stC(1)
-    stL(1)
     stPV(0)
     stT(2)
     stC(2)
-    stL(2)
     stPV(1)
     stPV(2)
     for b in range(3):
         stF(b)
+    for name in ("s0", "s1"):
+        if name in calls:
+            for t in calls[name]:
+                need(g, nn("sM", t["blk"]), nn("sE", t["blk"]))
+            emit(name)
     for b in range(3):
         if "o%d" % b in calls:
-            need(g, nn("sM", b), nn("sF", b))
+            need(g, nn("sF", b))
             emit("o%d" % b)
 
     if isrank:
         need(dv, "id")
         need(ac, "id")
+        order = [KINDS.index(x) for x in (("own", "mate", "diag", "plane") if core == me["PR"] else KINDS)]
+        mine = [b for b, (owner, _s) in enumerate(blocks) if owner == core]
+        cm = [T.sf[:, 8 + k:9 + k] for k in range(2)]
+        cs = [T.sf[:, 10 + k:11 + k] for k in range(2)]
+        cr = [T.sf[:, 12 + k:13 + k] for k in range(2)]
+        ce = [T.sf[:, 16 + 4 * k:20 + 4 * k] for k in range(2)]
+        cl = [T.sf[:, 24 + 4 * k:28 + 4 * k] for k in range(2)]
+        nm4 = [T.st[:, 16 * k:16 * k + 13:4] for k in range(2)]
+        l4 = [T.st[:, 16 * k + 1:16 * k + 14:4] for k in range(2)]
+        sdeps = [["sa%d" % k] + [nn(x, b) for b in mine if k == h for x in ("sM", "sE")] for k in range(2)]
         for k in range(2):
-            o, c, dg, Yk = T["oin%d" % k], "c%d" % k, T["dg%d" % k], T["Y%d" % k]
-            deps = ["oa%d" % k]
-            for b, (owner, _s) in enumerate(blocks):
-                if owner == core and k == h:
-                    deps += [nn("sM", b), nn("sF", b)]
-            cm, cs, cr = T.sf[:, 8 + k:9 + k], T.sf[:, 10 + k:11 + k], T.sf[:, 12 + k:13 + k]
-            ce, cl = T.sf[:, 16 + 4 * k:20 + 4 * k], T.sf[:, 24 + 4 * k:28 + 4 * k]
-            nm4, l4 = o[:, 128:537:136], o[:, 129:538:136]
-            need(dv, *deps)
-            inc(dv.tensor_reduce(cm, nm4, X, A.min), c)
-            need(ac, *deps)
-            need(ac, c)
-            inc(ac.activation(ce, nm4, Exp, bias=cm, scale=-1.0), c)
-            need(ac, c)
-            need(dv, c)
-            need(pe, *deps)
-            for n, i in enumerate((2, 0, 3, 1)):
+            need(dv, *sdeps[k])
+            inc(dv.tensor_reduce(cm[k], nm4[k], X, A.min), "c%d" % k)
+        for k in range(2):
+            need(ac, *sdeps[k])
+            need(ac, "c%d" % k)
+            inc(ac.activation(ce[k], nm4[k], Exp, bias=cm[k], scale=-1.0), "c%d" % k)
+        for k in range(2):
+            need(dv, "c%d" % k)
+            need(ac, "c%d" % k)
+            for n, i in enumerate(order):
                 col = T.sf[:, 16 + 4 * k + i:17 + 4 * k + i]
-                d = dg[:, i * 128:(i + 1) * 128]
-                if i >= 2:
+                d = T["dg%d" % k][:, i * 128:(i + 1) * 128]
+                if n < 2:
                     inc(dv.tensor_scalar(d, T.ident[:], col, None, A.mult), "g%d%d" % (k, i))
                 else:
                     inc(ac.activation(d, T.ident[:], Copy, scale=col), "g%d%d" % (k, i))
-                need(pe, "g%d%d" % (k, i))
-                inc(pe.matmul(Yk[:, 0:128], d, o[:, i * 136:i * 136 + 128], start=(n == 0), stop=(n == 3)), "y%d" % k)
-            inc(dv.tensor_tensor(cl, ce, l4, A.mult), c)
-            need(dv, c)
-            inc(dv.tensor_reduce(cs, cl, X, A.add), c)
-            need(dv, c)
-            inc(dv.reciprocal(cr, cs), c)
-            need(dv, c, "y%d" % k)
-            inc(dv.tensor_scalar(T.ysb[:, k * 128:k * 128 + 128], Yk[:, 0:128], cr, None, A.mult), c)
-            need(sy, c)
-            inc(sy.dma_start(T.y[:, k * 128:k * 128 + 128], T.ysb[:, k * 128:k * 128 + 128]), "st", 16)
+        for k in range(2):
+            inc(dv.tensor_tensor(cl[k], ce[k], l4[k], A.mult), "c%d" % k)
+        for k in range(2):
+            need(dv, "c%d" % k)
+            inc(dv.tensor_reduce(cs[k], cl[k], X, A.add), "c%d" % k)
+        for k in range(2):
+            need(dv, "c%d" % k)
+            inc(dv.reciprocal(cr[k], cs[k]), "c%d" % k)
+        for n, i in enumerate(order):
+            for k in range(2):
+                need(pe, "g%d%d" % (k, i), "oa%d%d" % (k, i))
+                if k == h and i == slot:
+                    need(pe, *[nn("sF", b) for b in mine])
+                inc(pe.matmul(T["Y%d" % k][:, 0:128], T["dg%d" % k][:, i * 128:(i + 1) * 128],
+                              T["oin%d" % k][:, i * 128:(i + 1) * 128], start=(n == 0), stop=(n == 3)), "y%d" % k)
+        need(dv, "c0", "y0")
+        inc(dv.tensor_scalar(T.ysb[:, 0:128], T.Y0[:, 0:128], cr[0], None, A.mult), "fin")
+        need(ac, "c1", "y1")
+        inc(ac.activation(T.ysb[:, 128:256], T.Y1[:, 0:128], Copy, scale=cr[1]), "fin")
+        need(sy, "fin")
+        inc(sy.dma_start(T.y[:], T.ysb[:]), "st", 16)
 
     for n in sorted(tot):
         need(g, n)

from concourse.bass import DstId, RemoteDMATransfer
from concourse.mybir import AluOpType, AxisListType, ActivationFunctionType

BF, F32 = "bfloat16", "float32"
KINDS = ["own", "plane", "mate", "diag"]
SCRATCH = {
    "kvown": ("sbuf", [128, 2, 256], BF),
    "qs": ("sbuf", [128, 256], BF),
    "kv": ("sbuf", [128, 3 * 256], BF),
    "qin": ("sbuf", [128, 3 * 128], BF),
    "qrel": ("sbuf", [128, 256], BF),
    "dif": ("sbuf", [128, 128], BF),
    "sq": ("sbuf", [128, 128], BF),
    "ident": ("sbuf", [128, 128], BF),
    "sf": ("sbuf", [128, 48], F32),
    "ss": ("sbuf", [128, 12], F32),
    "st": ("sbuf", [128, 32], F32),
    "ysb": ("sbuf", [128, 256], BF),
}
for _b in range(3):
    SCRATCH["os%d" % _b] = ("sbuf", [128, 128], BF)
    SCRATCH["p%d" % _b] = ("sbuf", [128, 384], BF)
    SCRATCH["pt%d" % _b] = ("sbuf", [128, 384], BF)
    SCRATCH["S%d" % _b] = ("psum", [128, 512], F32)
    SCRATCH["PT%d" % _b] = ("psum", [128, 1024], BF)
for _k in range(2):
    SCRATCH["oin%d" % _k] = ("sbuf", [128, 4 * 128], BF)
    SCRATCH["dg%d" % _k] = ("sbuf", [128, 512], BF)
    SCRATCH["Y%d" % _k] = ("psum", [128, 512], F32)

SEMAPHORES = ["ld_kv", "ld_q", "kl", "qp", "qn0", "qn1", "qx", "sa0", "sa1", "snd", "st", "on", "sq", "id", "fin"]
for _b in range(3):
    SEMAPHORES += ["%s%d" % (s, _b) for s in ("sS", "sM", "sE", "sT", "sC", "sO", "sF")]
for _k in range(2):
    SEMAPHORES += ["c%d" % _k, "y%d" % _k] + ["g%d%d" % (_k, i) for i in range(4)] + ["oa%d%d" % (_k, i) for i in range(4)]


def _bits(m):
    return [e for e in range(m.bit_length()) if (m >> e) & 1]


def _plan(T, topo):
    cores = list(T.cores)
    chips = sorted(set(topo.chip(c) for c in cores))
    P = {}
    for X in chips:
        ranks = [c for c in cores if topo.chip(c) == X]
        mate = [Y for Y in chips if topo.mates(X, Y)][0]
        plane = [Y for Y in chips if topo.same_plane(X, Y)][0]
        diag = [Y for Y in chips if topo.mates(plane, Y)][0]
        probe = [c for c in cores if topo.chip(c) == mate][0]
        onchip = [c for c in range(topo.CHIPS * topo.CORES_PER_CHIP) if topo.chip(c) == X]
        owners = [c for c in onchip if topo.may_write(c, probe)]
        NP = [r for r in ranks if r not in owners]
        PR = [r for r in ranks if r in owners][0]
        W, relay = [], []
        for h in range(2):
            dd = topo.die(NP[h])
            od = [c for c in owners if topo.die(c) == dd]
            nd = [c for c in onchip if topo.die(c) == dd and c not in owners and c != NP[h]]
            free = [c for c in od if c != PR]
            mt, dg = (PR, free[0]) if PR in od else (free[0], free[1])
            W.append({"own": NP[h], "plane": nd[0], "mate": mt, "diag": dg})
            relay.append([(free[0], ["mate"]), (free[1], ["diag"])] if len(free) > 1 else [(free[0], ["diag", "mate"])])
        P[X] = dict(chip=X, own=X, ranks=ranks, mate=mate, plane=plane, diag=diag, NP=NP, PR=PR, W=W, relay=relay)
    return P


def _role(c, P, topo):
    X = topo.chip(c)
    if X not in P:
        return None
    for h in range(2):
        for kind in KINDS:
            if P[X]["W"][h][kind] == c:
                return (h, kind)
    return None


def _blocks(c, P, topo):
    me = P[topo.chip(c)]
    h, kind = _role(c, P, topo)
    S = P[me[kind]]
    if kind == "own":
        return [(S["PR"], "qp"), (S["NP"][1 - h], "qx"), (S["NP"][h], "ld_q")]
    if kind == "plane":
        return [(S["NP"][0], "qn0"), (S["NP"][1], "qn1"), (S["PR"], "qp")]
    return [(S["PR"], "qp"), (S["NP"][0], "qn0"), (S["NP"][1], "qn1")]


def _qdst(w, owner, P, topo):
    b = [o for o, _s in _blocks(w, P, topo)].index(owner)
    return (w, "qin", b * 128, b * 128 + 128)


def _sends(c, P, topo):
    me = P[topo.chip(c)]
    M, PL, D = P[me["mate"]], P[me["plane"]], P[me["diag"]]
    far = {"mate": M, "diag": D}
    h, kind = _role(c, P, topo)
    lo = _bits(topo.mask(c, PL["ranks"][0]))
    on = _bits(topo.mask(c, [w for w in me["W"][0].values() if w != c][0]))
    hi = [e for e in on if e not in lo]
    hl, hh = len(lo) // 2, len(hi) // 2
    calls = {}
    if c in me["ranks"]:
        r = me["ranks"].index(c)
        t = []
        for k in range(2):
            src = ("qs", k * 128, k * 128 + 128)
            if c == me["PR"]:
                t.append(dict(src=src, dsts=[_qdst(w, c, P, topo) for w in
                                             (M["W"][k]["mate"], D["W"][k]["diag"], PL["W"][k]["plane"])],
                              sem="qp", eng=lo[k * hl:(k + 1) * hl]))
                t.append(dict(src=src, dsts=[_qdst(me["W"][k]["own"], c, P, topo)], sem="qp", eng=hi[k * hh:(k + 1) * hh]))
            else:
                if k != h:
                    t.append(dict(src=src, dsts=[_qdst(me["W"][k]["own"], c, P, topo)], sem="qx", eng=hi))
                t.append(dict(src=src, dsts=[_qdst(PL["W"][k]["plane"], c, P, topo)], sem="qn%d" % h,
                              eng=lo[k * hl:(k + 1) * hl]))
        if c != me["PR"]:
            calls["qr"] = [dict(src=("qs", 0, 256), dsts=[(rc, "qrel", 0, 256) for rc, _j in me["relay"][h]], sem="qx", eng=hi)]
        calls["q"] = t
        t = []
        for k in range(2):
            d = [me["W"][k][x] for x in KINDS if me["W"][k][x] != c]
            t.append(dict(src=("kvown", k * 256, k * 256 + 256), dsts=[(w, "kv", r * 256, (r + 1) * 256) for w in d],
                          sem="kl", eng=lo if len(d) == 3 else hi))
        calls["kv"] = t
    for j in range(2):
        for rc, jobs in me["relay"][j]:
            if rc == c:
                calls["qrel"] = [dict(src=("qrel", k * 128, k * 128 + 128),
                                      dsts=[_qdst(far[x]["W"][k][x], me["NP"][j], P, topo) for x in jobs],
                                      sem="qn%d" % j, eng=lo[k * hl:(k + 1) * hl]) for k in range(2)]
    slot = KINDS.index(kind)
    rem = [(b, o) for b, (o, _s) in enumerate(_blocks(c, P, topo)) if o != c]
    for gi, grp in enumerate(([x for x in rem if x[0] == 0], [x for x in rem if x[0] > 0])):
        t = []
        for n, (b, o) in enumerate(grp):
            e = _bits(topo.mask(c, o))
            w = len(e) // len(grp)
            cc = 4 * (4 * h + slot)
            t.append(dict(src=("ss", 4 * b, 4 * b + 2), dsts=[(o, "st", cc, cc + 2)], sem="sa%d" % h,
                          eng=e[n * w:(n + 1) * w], blk=b))
        if t:
            calls["s%d" % gi] = t
    for b, owner in rem:
        calls["o%d" % b] = [dict(src=("os%d" % b, 0, 128), dsts=[(owner, "oin%d" % h, slot * 128, slot * 128 + 128)],
                                 sem="oa%d%d" % (h, slot), eng=_bits(topo.mask(c, owner)))]
    return calls


def rank_program(g, core, T, topo):
    P = _plan(T, topo)
    role = _role(core, P, topo)
    if role is None:
        return
    h, kind = role
    me = P[topo.chip(core)]
    isrank = core in me["ranks"]
    blocks = _blocks(core, P, topo)
    calls = _sends(core, P, topo)
    pe, dv, ac, sy = g.tensor, g.vector, g.scalar, g.sync
    Exp, Copy, X = ActivationFunctionType.Exp, ActivationFunctionType.Copy, AxisListType.X
    A = AluOpType

    tot = {}
    for Y in P:
        for k in range(2):
            for w in P[Y]["W"][k].values():
                if w == core:
                    continue
                for trs in _sends(w, P, topo).values():
                    for t in trs:
                        for d in t["dsts"]:
                            if d[0] == core:
                                tot[t["sem"]] = tot.get(t["sem"], 0) + len(t["eng"])

    def S(n):
        return T.sem[n]

    def inc(ins, n, k=1):
        ins.then_inc(S(n), k)
        tot[n] = tot.get(n, 0) + k

    def need(q, *names):
        for n in names:
            if tot.get(n, 0) > 0:
                q.wait_ge(S(n), tot[n])

    def emit(name):
        trs = []
        for t in calls[name]:
            b, c0, c1 = t["src"]
            src = T.kvown[:, c0 // 256, :] if b == "kvown" else T[b][:, c0:c1]
            ids, dsts = [], []
            for (dc, db, d0, d1) in t["dsts"]:
                rid, pid, _se = topo.addr(dc)
                ids.append(DstId(rid=rid, pnc=pid))
                dsts.append(T[db][:, d0:d1])
            trs.append(RemoteDMATransfer(dst_ids=ids, dma_engine_mask=sum(1 << e for e in t["eng"]), remote_sem=S(t["sem"]),
                                         srcs=[src], dsts=dsts, alu_op=0))
            tot["snd"] = tot.get("snd", 0) + len(t["eng"])
        g.remote_dma_fused(trs, local_sem=S("snd"))

    if isrank:
        inc(sy.dma_start(T.qs[:], T.q[:]), "ld_q", 16)
        inc(ac.dma_start(T.kvown[:, :, 0:128], T.k[:]), "ld_kv", 16)
        inc(sy.dma_start(T.kvown[:, :, 128:256], T.v[:]), "ld_kv", 16)
    inc(g.iota(T.dif[:], [[-1, 128]], 0, 1, allow_small_or_imprecise_dtypes=True), "on")
    need(dv, "on")
    inc(dv.tensor_tensor(T.sq[:], T.dif[:], T.dif[:], A.mult), "sq")
    need(ac, "sq")
    inc(ac.activation(T.ident[:], T.sq[:], Exp, scale=-100.0), "id")
    if isrank:
        need(g, "ld_q")
        if "qr" in calls:
            emit("qr")
        emit("q")
        need(g, "ld_kv")
        emit("kv")
    if "qrel" in calls:
        need(g, "qx")
        emit("qrel")

    def Kap(s):
        return T.kvown[:, h, 0:128] if me["ranks"][s] == core else T.kv[:, s * 256:s * 256 + 128]

    def Vap(s):
        return T.kvown[:, h, 128:256] if me["ranks"][s] == core else T.kv[:, s * 256 + 128:s * 256 + 256]

    slot = KINDS.index(kind)
    Q, OUT, NM, LS = [], [], [], []
    for b, (owner, _s) in enumerate(blocks):
        if owner == core:
            cc = 4 * (4 * h + slot)
            Q.append(T.qs[:, h * 128:h * 128 + 128])
            OUT.append(T["oin%d" % h][:, slot * 128:slot * 128 + 128])
            NM.append(T.st[:, cc:cc + 1])
            LS.append(T.st[:, cc + 1:cc + 2])
        else:
            Q.append(T.qin[:, b * 128:b * 128 + 128])
            OUT.append(T["os%d" % b][:])
            NM.append(T.ss[:, 4 * b:4 * b + 1])
            LS.append(T.ss[:, 4 * b + 1:4 * b + 2])

    def nn(s, b):
        return "%s%d" % (s, b)

    def stS(b):
        need(pe, blocks[b][1], "kl", "ld_kv")
        for j in range(3):
            inc(pe.matmul(T[nn("S", b)][:, j * 128:(j + 1) * 128], Q[b], Kap(j), start=True, stop=True), nn("sS", b))

    def stM(b):
        need(dv, nn("sS", b))
        inc(dv.tensor_reduce(NM[b], T[nn("S", b)][:, 0:384], X, A.max, negate=True), nn("sM", b))

    def stE(b):
        need(ac, nn("sS", b), nn("sM", b))
        inc(ac.activation(T[nn("p", b)][:], T[nn("S", b)][:, 0:384], Exp, bias=NM[b], scale=1.0,
                          accum_out=LS[b]), nn("sE", b))

    def stT(b):
        need(pe, nn("sE", b), "id")
        for j in range(3):
            inc(pe.transpose(T[nn("PT", b)][:, j * 128:(j + 1) * 128], T[nn("p", b)][:, j * 128:(j + 1) * 128], T.ident[:]),
                nn("sT", b))

    def stC(b):
        need(dv, nn("sT", b))
        inc(dv.tensor_copy(T[nn("pt", b)][:], T[nn("PT", b)][:, 0:384]), nn("sC", b))

    def stPV(b):
        need(pe, nn("sC", b))
        for j in range(3):
            inc(pe.matmul(T[nn("S", b)][:, 0:128], T[nn("pt", b)][:, j * 128:(j + 1) * 128], Vap(j), start=(j == 0),
                          stop=(j == 2)), nn("sO", b))

    def stF(b):
        need(ac, nn("sO", b))
        inc(ac.activation(OUT[b], T[nn("S", b)][:, 0:128], Copy), nn("sF", b))

    for st in (stS, stM, stE):
        for b in range(3):
            st(b)
    stT(0)
    stT(1)
    stC(0)
    stC(1)
    stPV(0)
    stT(2)
    stC(2)
    stPV(1)
    stPV(2)
    for b in range(3):
        stF(b)
    for name in ("s0", "s1"):
        if name in calls:
            for t in calls[name]:
                need(g, nn("sM", t["blk"]), nn("sE", t["blk"]))
            emit(name)
    for b in range(3):
        if "o%d" % b in calls:
            need(g, nn("sF", b))
            emit("o%d" % b)

    if isrank:
        need(dv, "id")
        need(ac, "id")
        order = [KINDS.index(x) for x in (("own", "mate", "diag", "plane") if core == me["PR"] else KINDS)]
        mine = [b for b, (owner, _s) in enumerate(blocks) if owner == core]
        cm = [T.sf[:, 8 + k:9 + k] for k in range(2)]
        cs = [T.sf[:, 10 + k:11 + k] for k in range(2)]
        cr = [T.sf[:, 12 + k:13 + k] for k in range(2)]
        ce = [T.sf[:, 16 + 4 * k:20 + 4 * k] for k in range(2)]
        cl = [T.sf[:, 24 + 4 * k:28 + 4 * k] for k in range(2)]
        nm4 = [T.st[:, 16 * k:16 * k + 13:4] for k in range(2)]
        l4 = [T.st[:, 16 * k + 1:16 * k + 14:4] for k in range(2)]
        sdeps = [["sa%d" % k] + [nn(x, b) for b in mine if k == h for x in ("sM", "sE")] for k in range(2)]
        for k in range(2):
            need(dv, *sdeps[k])
            inc(dv.tensor_reduce(cm[k], nm4[k], X, A.min), "c%d" % k)
        for k in range(2):
            need(ac, *sdeps[k])
            need(ac, "c%d" % k)
            inc(ac.activation(ce[k], nm4[k], Exp, bias=cm[k], scale=-1.0), "c%d" % k)
        for k in range(2):
            need(dv, "c%d" % k)
            need(ac, "c%d" % k)
            for n, i in enumerate(order):
                col = T.sf[:, 16 + 4 * k + i:17 + 4 * k + i]
                d = T["dg%d" % k][:, i * 128:(i + 1) * 128]
                if n < 2:
                    inc(dv.tensor_scalar(d, T.ident[:], col, None, A.mult), "g%d%d" % (k, i))
                else:
                    inc(ac.activation(d, T.ident[:], Copy, scale=col), "g%d%d" % (k, i))
        for k in range(2):
            inc(dv.tensor_tensor(cl[k], ce[k], l4[k], A.mult), "c%d" % k)
        for k in range(2):
            need(dv, "c%d" % k)
            inc(dv.tensor_reduce(cs[k], cl[k], X, A.add), "c%d" % k)
        for k in range(2):
            need(dv, "c%d" % k)
            inc(dv.reciprocal(cr[k], cs[k]), "c%d" % k)
        for n, i in enumerate(order):
            for k in range(2):
                need(pe, "g%d%d" % (k, i), "oa%d%d" % (k, i))
                if k == h and i == slot:
                    need(pe, *[nn("sF", b) for b in mine])
                inc(pe.matmul(T["Y%d" % k][:, 0:128], T["dg%d" % k][:, i * 128:(i + 1) * 128],
                              T["oin%d" % k][:, i * 128:(i + 1) * 128], start=(n == 0), stop=(n == 3)), "y%d" % k)
        need(dv, "c0", "y0")
        inc(dv.tensor_scalar(T.ysb[:, 0:128], T.Y0[:, 0:128], cr[0], None, A.mult), "fin")
        need(ac, "c1", "y1")
        inc(ac.activation(T.ysb[:, 128:256], T.Y1[:, 0:128], Copy, scale=cr[1]), "fin")
        need(sy, "fin")
        inc(sy.dma_start(T.y[:], T.ysb[:]), "st", 16)

    for n in sorted(tot):
        need(g, n)
